import numpy as np, ml_dtypes
CORES = [56,61,80,85]
N = 4
import mx_ref
NC, G = 128, 4
C = np.float32(0.029)
BF = ml_dtypes.bfloat16
def cut(t, i, w=512):
    return t[:, w * i:w * i + w]
def tile(rs):
    return np.stack(rs, axis=2).reshape(128, -1).astype(BF)
def layer(w, X):
    out = []
    for i in range(G):
        for t in range(len(X)):
            p = mx_ref.matmul(mx_ref.quantize(cut(w, len(X) * i + t)), X[t])
            z = p if t == 0 else z + p
        out.append(z)
    return out
def act(Z):
    return [np.maximum(z, 0) * C for z in Z]
def pick(b):
    s = np.zeros((128, 128, 4), np.float32)
    s[np.arange(128), np.arange(128), b] = 1.0
    return mx_ref.quantize(s.reshape(128, 512).astype(BF))
def setup_inputs(rng):
    def f(*shape):
        return mx_ref.flush((rng.standard_normal(shape, dtype=np.float32) * np.exp2(rng.integers(-2, 3, shape[:-1] + (1,)))).astype(BF))
    return {"x": f(N, 128, 4 * NC), "w1": f(N, 128, G * 512), "w2": f(N, 128, 512), "a": f(N, 128, G * 512), "b": f(N, 128, N * 4 * NC)}
def setup_inputs_blocks(rng):
    d = setup_inputs(rng)
    for k in ("x", "w1", "w2", "a", "b"): d[k] = mx_ref.spread(d[k], rng, 2)
    return d
def setup_inputs_wide(rng):
    d = setup_inputs(rng)
    for k in ("x", "w1", "w2", "a", "b"): d[k] = mx_ref.flush((d[k].astype(np.float32) * np.exp2(rng.integers(-6, 7, (N, 1, 1))).astype(np.float32)).astype(BF))
    return d
def setup_inputs_zeros(rng):
    d = setup_inputs(rng); v = d["x"].reshape(N, 128, -1, 4).copy()
    v[np.broadcast_to((rng.random((N, 1, v.shape[2], 1)) < 0.33), v.shape)] = 0
    d["x"] = v.reshape(d["x"].shape)
    return d
def reference(x, w1, w2, a, b):
    H = [mx_ref.quantize(tile(act(layer(w1[j], [mx_ref.quantize(x[j])])))) for j in range(N)]
    y = np.zeros((N, 128, N * NC), np.float32)
    for r in range(N):
        qw = mx_ref.quantize(w2[r])
        for j in range(N):
            y[r][:, NC * j:NC * j + NC] = mx_ref.matmul(qw, H[j])
    S = [pick(t) for t in range(4)]
    z = np.zeros((N, 128, NC, 4), np.float32)
    for c in range(N):
        for r in range(N):
            q = mx_ref.quantize(tile(act(layer(a[r], [mx_ref.quantize(cut(b[r], c, 4 * NC))]))))
            p = np.stack([mx_ref.matmul(S[t], q) for t in range(4)], axis=2)
            z[c] = p if r == 0 else z[c] + p
    return {"y": y, "z": z.reshape(N, 128, 4 * NC)}

@@ -1,0 +1,261 @@
+from concourse.bass import DstId, RemoteDMATransfer
+from concourse.mybir import dt, AluOpType, ActivationFunctionType
+
+NC = 128
+W = 4 * NC
+FACTOR = 0.029
+
+SCRATCH = {
+    "ta": ("sbuf", [128, 4 * W], "bfloat16"),
+    "tb1": ("sbuf", [128, 2 * W], "bfloat16"),
+    "tb2": ("sbuf", [128, 2 * W], "bfloat16"),
+    "tw1": ("sbuf", [128, 4 * W], "bfloat16"),
+    "tx": ("sbuf", [128, W], "bfloat16"),
+    "tw2": ("sbuf", [128, W], "bfloat16"),
+    "ones": ("sbuf", [128, W + 4], "bfloat16"),
+    "eye": ("sbuf", [128, W + 4], "bfloat16"),
+    "tg1": ("sbuf", [128, 2 * W], "bfloat16"),
+    "tg2": ("sbuf", [128, 2 * W], "bfloat16"),
+    "th": ("sbuf", [128, W], "bfloat16"),
+    "zt": ("sbuf", [128, W], "float32"),
+    "yt1": ("sbuf", [128, 2 * NC], "float32"),
+    "yt2": ("sbuf", [128, 2 * NC], "float32"),
+    "P0": ("psum", [128, 2048], "float32"),
+    "P1": ("psum", [128, 2048], "float32"),
+}
+for _n, _w in (("a", 4), ("b1", 2), ("b2", 2), ("w1", 4), ("x", 1), ("w2", 1), ("s", 4),
+               ("g1", 2),
+               ("o", 3),
+               ("n", 2),
+               ("lg0", 1), ("lg1", 1), ("lh0", 1), ("lh1", 1),
+               ("rg", 1), ("rh", 1)):
+    SCRATCH["q" + _n] = ("sbuf", [128, _w * NC], "float8_e4m3fn_x4")
+    SCRATCH["p" + _n] = ("sbuf", [128, _w * NC], "uint8")
+
+SEMAPHORES = (["l_" + n for n in ("a", "b1", "b2", "w1", "x", "w2")]
+              + ["k_" + n for n in ("a", "b1", "b2", "w1", "x", "w2", "s", "g1", "g2", "h")]
+              + ["ones", "eye", "act_g1", "act_g2", "act_h", "cy1", "cy2", "cz", "stored", "sent"]
+              + ["m_%s%d" % (n, b) for n in ("g1", "g2", "h", "z", "y") for b in range(4)]
+              + ["an", "ag0", "ag1", "ah0", "ah1", "rgc", "rgp", "rhc", "rhp", "k_hb", "k_gb"])
+
+
+def engines(topo, src, dst):
+    m = topo.mask(src, dst)
+    return [1 << i for i in range(m.bit_length()) if (m >> i) & 1]
+
+
+def dest(topo, c):
+    rid, pid, _ = topo.addr(c)
+    return DstId(rid=rid, pnc=pid)
+
+
+def plan(T, topo):
+    cores = list(T.cores)
+    ranks = range(len(cores))
+    P = []
+    for r in ranks:
+        c = cores[r]
+        near = [s for s in ranks if topo.chip(cores[s]) == topo.chip(c)]
+        far = [s for s in ranks if s not in near]
+        nb = [s for s in near if s != r][0]
+        P.append({"near": near, "far": far, "nb": nb})
+    return P
+
+
+def relays(T, topo, r, far, sim):
+    c = T.cores[r]
+    found = [k for k in sim if topo.chip(k) == topo.chip(c) and topo.die(k) == topo.die(c) and k not in T.cores
+             and all(topo.may_write(k, T.cores[f]) for f in far)]
+    return found[:len(far)]
+
+
+def rank_program(g, core, T, topo):
+    P = plan(T, topo)
+    sim = range(max(T.cores) + 16)
+    R = {}
+    for r in range(len(T.cores)):
+        R[r] = relays(T, topo, r, P[r]["far"], [k for k in sim if topo.chip(k) == topo.chip(T.cores[r])])
+    rank = T.rank_of(core)
+    if rank is not None:
+        rank_core(g, core, rank, T, topo, P, R)
+        return
+    for r in R:
+        if core in R[r]:
+            relay_core(g, core, r, R[r].index(core), T, topo, P)
+
+
+def u8(ap):
+    return ap.bitcast(dt.uint8)
+
+
+def relay_core(g, core, r, k, T, topo, P):
+    d = P[r]["far"][k]
+    to = T.cores[d]
+    me = P[d]["far"].index(r)
+    eng = engines(topo, core, to)
+    mask, n = sum(eng), len(eng)
+    rid, pid, _ = topo.addr(to)
+    half = len(engines(topo, T.cores[r], core)) // 2
+    for t in ("g", "h"):
+        arrive = T.sem["a%s%d" % (t, me)]
+        g.wait_ge(T.sem["r%sc" % t], half)
+        g.remote_dma(u8(T["ql%s%d" % (t, me)][:, 0:NC]), u8(T["qr" + t][:, 0:NC]), arrive, T.sem.sent, pid, rid, mask)
+        g.wait_ge(T.sem["r%sp" % t], half)
+        g.remote_dma(T["pl%s%d" % (t, me)][:, 0:NC], T["pr" + t][:, 0:NC], arrive, T.sem.sent, pid, rid, mask)
+    g.wait_ge(T.sem.sent, 4 * n)
+
+
+def rank_core(g, core, rank, T, topo, P, R):
+    S = T.sem
+    near, far, nb = P[rank]["near"], P[rank]["far"], P[rank]["nb"]
+    helpers = R[rank]
+    v, s, t, y = g.vector, g.scalar, g.tensor, g.sync
+    RELU, COPY = ActivationFunctionType.Relu, ActivationFunctionType.Copy
+
+    if nb > rank:
+        og, oh, own, send = 0, 2, 0, 1
+    else:
+        og, oh, own, send = 1, 0, 2, 0
+    ng, nh = (0, 1) if rank > nb else (1, 0)
+
+    def cols(buf, i, n=1):
+        return T[buf][:, i * NC:(i + n) * NC]
+
+    f0, n0 = far[0], near[0]
+    y.dma_start(T.ta[:], T.a[:]).then_inc(S.l_a, 16)
+    s.dma_start(T.tb1[:], T.b[:, f0 * W:(f0 + 2) * W]).then_inc(S.l_b1, 16)
+    y.dma_start(T.tw1[:], T.w1[:]).then_inc(S.l_w1, 16)
+    s.dma_start(T.tx[:], T.x[:]).then_inc(S.l_x, 16)
+    y.wait_ge(S.l_a, 16)
+    y.dma_start(T.tb2[:], T.b[:, n0 * W:(n0 + 2) * W]).then_inc(S.l_b2, 16)
+    y.dma_start(T.tw2[:], T.w2[:]).then_inc(S.l_w2, 16)
+
+    v.memset(T.ones[:], 1.0).then_inc(S.ones, 1)
+    v.wait_ge(S.eye, 1)
+    for b in range(4):
+        v.quantize_mx(cols("qs", b), cols("ps", b), T.eye[:, 3 - b:3 - b + W]).then_inc(S.k_s, 1)
+
+    def quant(n, src):
+        v.wait_ge(S["l_" + n], 16)
+        v.quantize_mx(T["q" + n][:], T["p" + n][:], T[src][:]).then_inc(S["k_" + n], 1)
+
+    def act_v(n, bank, tile, width):
+        for b in (2, 3):
+            v.wait_ge(S["m_%s%d" % (n, b)], 1)
+            v.tensor_scalar(T[tile][:, b:4 * width:4], T[bank][:, 512 * b:512 * b + width], 0.0, FACTOR,
+                            AluOpType.max, AluOpType.mult).then_inc(S["act_" + n], 1)
+        v.wait_ge(S["act_" + n], 4)
+
+    def act_s(n, bank, tile, width):
+        for b in (0, 1):
+            s.wait_ge(S["m_%s%d" % (n, b)], 1)
+            s.activation(T[tile][:, b:4 * width:4], T[bank][:, 512 * b:512 * b + width], RELU,
+                         scale=FACTOR).then_inc(S["act_" + n], 1)
+
+    quant("a", "ta")
+    quant("b1", "tb1")
+    act_v("g1", "P0", "tg1", 2 * NC)
+    v.quantize_mx(T.qg1[:], T.pg1[:], T.tg1[:]).then_inc(S.k_g1, 1)
+    quant("w1", "tw1")
+    quant("x", "tx")
+    act_v("h", "P1", "th", NC)
+    v.quantize_mx(cols("qo", oh), cols("po", oh), T.th[:]).then_inc(S.k_h, 1)
+    quant("b2", "tb2")
+    act_v("g2", "P0", "tg2", 2 * NC)
+    v.quantize_mx(cols("qo", og, 2), cols("po", og, 2), T.tg2[:]).then_inc(S.k_g2, 1)
+    quant("w2", "tw2")
+
+    def layer(w, m, n, bank, width):
+        for b in range(4):
+            t.matmul_mx(T[bank][:, 512 * b:512 * b + width], cols("q" + w, b), cols("p" + w, b), T["q" + m][:], T["p" + m][:],
+                        True, True).then_inc(S["m_%s%d" % (n, b)], 1)
+
+    def unpack(q, p, first, last):
+        for b in range(4):
+            i = t.matmul_mx(T.P1[:, 512 * b:512 * b + NC], cols("qs", b), cols("ps", b), q, p, first, last)
+            if last:
+                i.then_inc(S["m_z%d" % b], 1)
+
+    def yblock(k, q, p):
+        t.matmul_mx(T.P0[:, 512 * k:512 * k + NC], T.qw2[:], T.pw2[:], q, p, True, True).then_inc(S["m_y%d" % k], 1)
+
+    t.wait_ge(S.k_a, 1)
+    t.wait_ge(S.k_b1, 1)
+    layer("a", "b1", "g1", "P0", 2 * NC)
+    t.wait_ge(S.k_w1, 1)
+    t.wait_ge(S.k_x, 1)
+    layer("w1", "x", "h", "P1", NC)
+    t.wait_ge(S.k_b2, 1)
+    t.wait_ge(S.act_g1, 4)
+    layer("a", "b2", "g2", "P0", 2 * NC)
+    t.wait_ge(S.k_s, 4)
+    t.wait_ge(S.act_h, 4)
+    t.wait_ge(S.k_g2, 1)
+    unpack(cols("qo", own), cols("po", own), True, False)
+    t.wait_ge(S.k_w2, 1)
+    t.wait_ge(S.act_g2, 4)
+    t.wait_ge(S.k_h, 1)
+    yblock(near.index(rank), cols("qo", oh), cols("po", oh))
+    every = len(engines(topo, core, T.cores[nb]))
+    off = len(engines(topo, helpers[0], T.cores[far[0]]))
+    t.wait_ge(S.an, 2 * every)
+    yblock(near.index(nb), cols("qn", nh), cols("pn", nh))
+    unpack(cols("qn", ng), cols("pn", ng), False, False)
+    for k in (0, 1):
+        t.wait_ge(S["ag%d" % k], 2 * off)
+        unpack(T["qlg%d" % k][:], T["plg%d" % k][:], False, k == 1)
+    for k in (0, 1):
+        t.wait_ge(S["ah%d" % k], 2 * off)
+        yblock(2 + k, T["qlh%d" % k][:], T["plh%d" % k][:])
+
+    act_s("g1", "P0", "tg1", 2 * NC)
+    act_s("h", "P1", "th", NC)
+    act_s("g2", "P0", "tg2", 2 * NC)
+
+    def out_s(sem, dst, src, done):
+        s.wait_ge(sem, 1)
+        s.activation(dst, src, COPY).then_inc(done, 1)
+
+    def out_v(sem, dst, src, done):
+        v.wait_ge(sem, 1)
+        v.tensor_copy(dst, src).then_inc(done, 1)
+
+    out_v(S.m_y0, T.yt1[:, 0:NC], T.P0[:, 0:NC], S.cy1)
+    out_s(S.m_y1, T.yt1[:, NC:2 * NC], T.P0[:, 512:512 + NC], S.cy1)
+    for b in range(4):
+        (out_s if b % 2 == 0 else out_v)(S["m_z%d" % b], T.zt[:, b:W:4], T.P1[:, 512 * b:512 * b + NC], S.cz)
+    out_v(S.m_y2, T.yt2[:, 0:NC], T.P0[:, 1024:1024 + NC], S.cy2)
+    out_s(S.m_y3, T.yt2[:, NC:2 * NC], T.P0[:, 1536:1536 + NC], S.cy2)
+
+    y.wait_ge(S.cy1, 2)
+    y.dma_start(T.y[:, n0 * NC:(n0 + 2) * NC], T.yt1[:]).then_inc(S.stored, 16)
+    y.wait_ge(S.cz, 4)
+    y.dma_start(T.z[:], T.zt[:]).then_inc(S.stored, 16)
+    y.wait_ge(S.cy2, 2)
+    y.dma_start(T.y[:, f0 * NC:(f0 + 2) * NC], T.yt2[:]).then_inc(S.stored, 16)
+    y.wait_ge(S.stored, 48)
+
+    g.wait_ge(S.ones, 1)
+    g.affine_select(T.eye[:], T.ones[:], [[-1, W + 4]], AluOpType.is_equal, 0.0, 3, 4).then_inc(S.eye, 1)
+
+    def to_relays(srcs, dst, sem):
+        tr = []
+        for k in (0, 1):
+            e = engines(topo, core, helpers[k])
+            h = len(e) // 2
+            tr.append(RemoteDMATransfer(dst_ids=[dest(topo, helpers[k])], dma_engine_mask=sum(e[k * h:(k + 1) * h]),
+                                        remote_sem=sem, src=srcs[k], dst=dst))
+        g.remote_dma_fused(tr, local_sem=S.sent)
+
+    g.wait_ge(S.k_g1, 1)
+    to_relays([u8(cols("qg1", k)) for k in (0, 1)], u8(T.qrg[:]), S.rgc)
+    to_relays([cols("pg1", k) for k in (0, 1)], T.prg[:], S.rgp)
+    g.wait_ge(S.k_h, 1)
+    to_relays([u8(cols("qo", oh))] * 2, u8(T.qrh[:]), S.rhc)
+    to_relays([cols("po", oh)] * 2, T.prh[:], S.rhp)
+    rid, pid, _ = topo.addr(T.cores[nb])
+    e = engines(topo, core, T.cores[nb])
+    g.wait_ge(S.k_g2, 1)
+    g.remote_dma(u8(T.qn[:]), u8(cols("qo", send, 2)), S.an, S.sent, pid, rid, sum(e))
+    g.remote_dma(T.pn[:], cols("po", send, 2), S.an, S.sent, pid, rid, sum(e))
+    g.wait_ge(S.sent, 6 * len(e))

@@ -5,38 +5,48 @@ NC = 128
 W = 4 * NC
 FACTOR = 0.029
 
+CFG = {
+    "sync": [("a", 0, 2), ("x", 0, 1), ("w1", 2, 2), ("l_a0", 16), ("bn", 0, 1), ("bo", 0, 1), ("w2", 0, 1)],
+    "scalar": [("bf", 0, 2), ("a", 2, 2), ("w1", 0, 2)],
+    "vec": [("s", "gift"), ("q", "bf", 0), ("q", "a", 0), ("q", "a", 2), ("q", "x", 0), ("q", "w1", 0), ("t", "gf"),
+            ("q", "w1", 2), ("r", "h", 2), ("t", "h"), ("q", "bn", 0), ("r", "gn", 1), ("r", "gn", 3), ("t", "gn"),
+            ("q", "bo", 0), ("s", "rest"), ("r", "go", 1), ("r", "go", 3), ("t", "go"), ("q", "w2", 0)],
+    "sca": [("r", "gf", 0), ("r", "gf", 1), ("r", "gf", 2), ("r", "gf", 3), ("r", "h", 0), ("r", "h", 1), ("r", "h", 3),
+            ("r", "gn", 0), ("r", "gn", 2), ("r", "go", 0), ("r", "go", 2)],
+    "ten": ["d own", "y own", "d nb", "y nb", "d 0", "d 1", "y 0", "y 1"],
+}
+TILES = {"a": 4, "bf": 2, "bn": 1, "bo": 1, "w1": 4, "x": 1, "w2": 1}
+MADE = {"gf": (2, "P0"), "gn": (1, "P0"), "go": (1, "P1"), "h": (1, "P1")}
+
 SCRATCH = {
-    "ta": ("sbuf", [128, 4 * W], "bfloat16"),
-    "tb1": ("sbuf", [128, 2 * W], "bfloat16"),
-    "tb2": ("sbuf", [128, 2 * W], "bfloat16"),
-    "tw1": ("sbuf", [128, 4 * W], "bfloat16"),
-    "tx": ("sbuf", [128, W], "bfloat16"),
-    "tw2": ("sbuf", [128, W], "bfloat16"),
     "ones": ("sbuf", [128, W + 4], "bfloat16"),
     "eye": ("sbuf", [128, W + 4], "bfloat16"),
-    "tg1": ("sbuf", [128, 2 * W], "bfloat16"),
-    "tg2": ("sbuf", [128, 2 * W], "bfloat16"),
-    "th": ("sbuf", [128, W], "bfloat16"),
     "zt": ("sbuf", [128, W], "float32"),
     "yt1": ("sbuf", [128, 2 * NC], "float32"),
     "yt2": ("sbuf", [128, 2 * NC], "float32"),
     "P0": ("psum", [128, 2048], "float32"),
     "P1": ("psum", [128, 2048], "float32"),
 }
-for _n, _w in (("a", 4), ("b1", 2), ("b2", 2), ("w1", 4), ("x", 1), ("w2", 1), ("s", 4),
-               ("g1", 2),
-               ("o", 3),
+for _n in TILES:
+    SCRATCH["t" + _n] = ("sbuf", [128, TILES[_n] * W], "bfloat16")
+for _n in MADE:
+    SCRATCH["t" + _n] = ("sbuf", [128, MADE[_n][0] * W], "bfloat16")
+for _n, _w in (("a", 4), ("bf", 2), ("bn", 1), ("bo", 1), ("w1", 4), ("x", 1), ("w2", 1), ("s", 4),
+               ("gf", 2),
+               ("o", 2),
+               ("go", 1),
                ("n", 2),
                ("lg0", 1), ("lg1", 1), ("lh0", 1), ("lh1", 1),
                ("rg", 1), ("rh", 1)):
     SCRATCH["q" + _n] = ("sbuf", [128, _w * NC], "float8_e4m3fn_x4")
     SCRATCH["p" + _n] = ("sbuf", [128, _w * NC], "uint8")
 
-SEMAPHORES = (["l_" + n for n in ("a", "b1", "b2", "w1", "x", "w2")]
-              + ["k_" + n for n in ("a", "b1", "b2", "w1", "x", "w2", "s", "g1", "g2", "h")]
-              + ["ones", "eye", "act_g1", "act_g2", "act_h", "cy1", "cy2", "cz", "stored", "sent"]
-              + ["m_%s%d" % (n, b) for n in ("g1", "g2", "h", "z", "y") for b in range(4)]
-              + ["an", "ag0", "ag1", "ah0", "ah1", "rgc", "rgp", "rhc", "rhp", "k_hb", "k_gb"])
+SEMAPHORES = (["l_%s%d" % (n, i) for n in TILES for i in range(TILES[n])]
+              + ["k_%s%d" % (n, i) for n in TILES for i in range(TILES[n])]
+              + ["k_s", "k_gift"] + ["k_" + n for n in MADE] + ["act_" + n for n in MADE]
+              + ["ones", "eye", "cy1", "cy2", "cz", "stored", "sent"]
+              + ["m_%s%d" % (n, b) for n in list(MADE) + ["z", "y"] for b in range(4)]
+              + ["as", "an", "ag0", "ag1", "ah0", "ah1", "rgc", "rgp", "rhc", "rhp"])
 
 
 def engines(topo, src, dst):
@@ -57,186 +67,201 @@ def plan(T, topo):
         c = cores[r]
         near = [s for s in ranks if topo.chip(cores[s]) == topo.chip(c)]
         far = [s for s in ranks if s not in near]
-        nb = [s for s in near if s != r][0]
-        P.append({"near": near, "far": far, "nb": nb})
+        found = [k for k in range(max(c - 16, 0), c + 16) if topo.chip(k) == topo.chip(c) and topo.die(k) == topo.die(c)
+                 and k not in cores and all(topo.may_write(k, cores[f]) for f in far)]
+        P.append({"near": near, "far": far, "nb": [s for s in near if s != r][0], "lack": 3 if r == near[0] else 0,
+                  "relays": found[:len(far)]})
     return P
-
-
-def relays(T, topo, r, far, sim):
-    c = T.cores[r]
-    found = [k for k in sim if topo.chip(k) == topo.chip(c) and topo.die(k) == topo.die(c) and k not in T.cores
-             and all(topo.may_write(k, T.cores[f]) for f in far)]
-    return found[:len(far)]
 
 
 def rank_program(g, core, T, topo):
     P = plan(T, topo)
-    sim = range(max(T.cores) + 16)
-    R = {}
-    for r in range(len(T.cores)):
-        R[r] = relays(T, topo, r, P[r]["far"], [k for k in sim if topo.chip(k) == topo.chip(T.cores[r])])
     rank = T.rank_of(core)
     if rank is not None:
-        rank_core(g, core, rank, T, topo, P, R)
+        rank_core(g, core, rank, T, topo, P)
         return
-    for r in R:
-        if core in R[r]:
-            relay_core(g, core, r, R[r].index(core), T, topo, P)
+    for r in range(len(P)):
+        if core in P[r]["relays"]:
+            relay_core(g, core, r, P[r]["relays"].index(core), T, topo, P)
 
 
 def u8(ap):
     return ap.bitcast(dt.uint8)
 
 
+def make_eye(g, T):
+    g.vector.memset(T.ones[:], 1.0).then_inc(T.sem.ones, 1)
+    g.wait_ge(T.sem.ones, 1)
+    g.affine_select(T.eye[:], T.ones[:], [[-1, W + 4]], AluOpType.is_equal, 0.0, 3, 4).then_inc(T.sem.eye, 1)
+
+
+def quant_s(g, T, b, sem):
+    g.vector.quantize_mx(T.qs[:, b * NC:(b + 1) * NC], T.ps[:, b * NC:(b + 1) * NC], T.eye[:, 3 - b:3 - b + W]).then_inc(sem, 1)
+
+
+def send(g, topo, to, mask, codes, planes, a, b, sem_c, sem_p, sent):
+    rid, pid, _ = topo.addr(to)
+    g.remote_dma(u8(codes[:, a:b]), u8(codes[:, a:b]), sem_c, sent, pid, rid, mask)
+    g.remote_dma(planes[:, a:b], planes[:, a:b], sem_p, sent, pid, rid, mask)
+
+
 def relay_core(g, core, r, k, T, topo, P):
+    S = T.sem
     d = P[r]["far"][k]
-    to = T.cores[d]
+    to, home, lack = T.cores[d], T.cores[r], P[r]["lack"]
     me = P[d]["far"].index(r)
     eng = engines(topo, core, to)
     mask, n = sum(eng), len(eng)
+    make_eye(g, T)
+    g.vector.wait_ge(S.eye, 1)
+    quant_s(g, T, lack, S.k_s)
+    g.wait_ge(S.k_s, 1)
+    c = lack * NC + NC // 2 + k * (NC // 4)
+    send(g, topo, home, mask, T.qs, T.ps, c, c + NC // 4, S["as"], S["as"], S.sent)
     rid, pid, _ = topo.addr(to)
-    half = len(engines(topo, T.cores[r], core)) // 2
+    half = len(engines(topo, home, core)) // 2
     for t in ("g", "h"):
-        arrive = T.sem["a%s%d" % (t, me)]
-        g.wait_ge(T.sem["r%sc" % t], half)
-        g.remote_dma(u8(T["ql%s%d" % (t, me)][:, 0:NC]), u8(T["qr" + t][:, 0:NC]), arrive, T.sem.sent, pid, rid, mask)
-        g.wait_ge(T.sem["r%sp" % t], half)
-        g.remote_dma(T["pl%s%d" % (t, me)][:, 0:NC], T["pr" + t][:, 0:NC], arrive, T.sem.sent, pid, rid, mask)
-    g.wait_ge(T.sem.sent, 4 * n)
+        arrive = S["a%s%d" % (t, me)]
+        g.wait_ge(S["r%sc" % t], half)
+        g.remote_dma(u8(T["ql%s%d" % (t, me)][:, 0:NC]), u8(T["qr" + t][:, 0:NC]), arrive, S.sent, pid, rid, mask)
+        g.wait_ge(S["r%sp" % t], half)
+        g.remote_dma(T["pl%s%d" % (t, me)][:, 0:NC], T["pr" + t][:, 0:NC], arrive, S.sent, pid, rid, mask)
+    g.wait_ge(S.sent, 6 * n)
 
 
-def rank_core(g, core, rank, T, topo, P, R):
+def rank_core(g, core, rank, T, topo, P):
     S = T.sem
-    near, far, nb = P[rank]["near"], P[rank]["far"], P[rank]["nb"]
-    helpers = R[rank]
+    near, far, nb, lack, helpers = [P[rank][k] for k in ("near", "far", "nb", "lack", "relays")]
+    gift = P[nb]["lack"]
     v, s, t, y = g.vector, g.scalar, g.tensor, g.sync
     RELU, COPY = ActivationFunctionType.Relu, ActivationFunctionType.Copy
-
-    if nb > rank:
-        og, oh, own, send = 0, 2, 0, 1
-    else:
-        og, oh, own, send = 1, 0, 2, 0
-    ng, nh = (0, 1) if rank > nb else (1, 0)
+    e_nb = engines(topo, core, T.cores[nb])
+    off = len(engines(topo, helpers[0], T.cores[far[0]]))
 
     def cols(buf, i, n=1):
         return T[buf][:, i * NC:(i + n) * NC]
 
-    f0, n0 = far[0], near[0]
-    y.dma_start(T.ta[:], T.a[:]).then_inc(S.l_a, 16)
-    s.dma_start(T.tb1[:], T.b[:, f0 * W:(f0 + 2) * W]).then_inc(S.l_b1, 16)
-    y.dma_start(T.tw1[:], T.w1[:]).then_inc(S.l_w1, 16)
-    s.dma_start(T.tx[:], T.x[:]).then_inc(S.l_x, 16)
-    y.wait_ge(S.l_a, 16)
-    y.dma_start(T.tb2[:], T.b[:, n0 * W:(n0 + 2) * W]).then_inc(S.l_b2, 16)
-    y.dma_start(T.tw2[:], T.w2[:]).then_inc(S.l_w2, 16)
+    where = {"gf": ("gf", 0), "gn": ("o", 1), "go": ("go", 0), "h": ("o", 0)}
+    source = {"a": (T.a, 0), "bf": (T.b, far[0]), "bn": (T.b, nb), "bo": (T.b, rank), "w1": (T.w1, 0), "x": (T.x, 0), "w2": (T.w2, 0)}
+    parts = [p for p in CFG["sync"] + CFG["scalar"] if len(p) == 3]
+    size = {(n, i): k for n, i, k in parts}
 
-    v.memset(T.ones[:], 1.0).then_inc(S.ones, 1)
-    v.wait_ge(S.eye, 1)
-    for b in range(4):
-        v.quantize_mx(cols("qs", b), cols("ps", b), T.eye[:, 3 - b:3 - b + W]).then_inc(S.k_s, 1)
+    def piece(n, tile):
+        return [(m, i) for m, i, k in parts if m == n and i <= tile < i + k][0]
 
-    def quant(n, src):
-        v.wait_ge(S["l_" + n], 16)
-        v.quantize_mx(T["q" + n][:], T["p" + n][:], T[src][:]).then_inc(S["k_" + n], 1)
+    def load(q, queue):
+        for p in queue:
+            if len(p) == 2:
+                q.wait_ge(S[p[0]], p[1])
+                continue
+            n, i, k = p
+            src, at = source[n]
+            q.dma_start(T["t" + n][:, i * W:(i + k) * W], src[:, (at + i) * W:(at + i + k) * W]).then_inc(S["l_%s%d" % (n, i)], 16)
 
-    def act_v(n, bank, tile, width):
-        for b in (2, 3):
-            v.wait_ge(S["m_%s%d" % (n, b)], 1)
-            v.tensor_scalar(T[tile][:, b:4 * width:4], T[bank][:, 512 * b:512 * b + width], 0.0, FACTOR,
-                            AluOpType.max, AluOpType.mult).then_inc(S["act_" + n], 1)
-        v.wait_ge(S["act_" + n], 4)
+    load(y, CFG["sync"])
+    load(s, CFG["scalar"])
+    make_eye(g, T)
 
-    def act_s(n, bank, tile, width):
-        for b in (0, 1):
-            s.wait_ge(S["m_%s%d" % (n, b)], 1)
-            s.activation(T[tile][:, b:4 * width:4], T[bank][:, 512 * b:512 * b + width], RELU,
-                         scale=FACTOR).then_inc(S["act_" + n], 1)
+    def result(q, n, b):
+        k, bank = MADE[n]
+        q.wait_ge(S["m_%s%d" % (n, b)], 1)
+        dst, src = T["t" + n][:, b:k * W:4], T[bank][:, 512 * b:512 * b + k * NC]
+        i = q.activation(dst, src, RELU, scale=FACTOR) if q is s else q.tensor_scalar(dst, src, 0.0, FACTOR, AluOpType.max, AluOpType.mult)
+        i.then_inc(S["act_" + n], 1)
 
-    quant("a", "ta")
-    quant("b1", "tb1")
-    act_v("g1", "P0", "tg1", 2 * NC)
-    v.quantize_mx(T.qg1[:], T.pg1[:], T.tg1[:]).then_inc(S.k_g1, 1)
-    quant("w1", "tw1")
-    quant("x", "tx")
-    act_v("h", "P1", "th", NC)
-    v.quantize_mx(cols("qo", oh), cols("po", oh), T.th[:]).then_inc(S.k_h, 1)
-    quant("b2", "tb2")
-    act_v("g2", "P0", "tg2", 2 * NC)
-    v.quantize_mx(cols("qo", og, 2), cols("po", og, 2), T.tg2[:]).then_inc(S.k_g2, 1)
-    quant("w2", "tw2")
+    for op in CFG["vec"]:
+        n = op[1]
+        if op[0] == "s":
+            v.wait_ge(S.eye, 1)
+            if n == "gift":
+                quant_s(g, T, gift, S.k_gift)
+            else:
+                for b in range(4):
+                    if b not in (gift, lack):
+                        quant_s(g, T, b, S.k_s)
+        elif op[0] == "q":
+            i = op[2]
+            k = size[n, i]
+            v.wait_ge(S["l_%s%d" % (n, i)], 16)
+            v.quantize_mx(cols("q" + n, i, k), cols("p" + n, i, k), T["t" + n][:, i * W:(i + k) * W]).then_inc(S["k_%s%d" % (n, i)], 1)
+        elif op[0] == "r":
+            result(v, n, op[2])
+        else:
+            buf, i = where[n]
+            v.wait_ge(S["act_" + n], 4)
+            v.quantize_mx(cols("q" + buf, i, MADE[n][0]), cols("p" + buf, i, MADE[n][0]), T["t" + n][:]).then_inc(S["k_" + n], 1)
+    for op in CFG["sca"]:
+        result(s, op[1], op[2])
 
-    def layer(w, m, n, bank, width):
+    def need(n, tile):
+        t.wait_ge(S["k_%s%d" % piece(n, tile)], 1)
+
+    def layer(w, m, n):
+        width, bank = MADE[n][0] * NC, MADE[n][1]
+        need(m, 0)
         for b in range(4):
+            need(w, b)
             t.matmul_mx(T[bank][:, 512 * b:512 * b + width], cols("q" + w, b), cols("p" + w, b), T["q" + m][:], T["p" + m][:],
                         True, True).then_inc(S["m_%s%d" % (n, b)], 1)
 
-    def unpack(q, p, first, last):
-        for b in range(4):
-            i = t.matmul_mx(T.P1[:, 512 * b:512 * b + NC], cols("qs", b), cols("ps", b), q, p, first, last)
-            if last:
-                i.then_inc(S["m_z%d" % b], 1)
-
-    def yblock(k, q, p):
-        t.matmul_mx(T.P0[:, 512 * k:512 * k + NC], T.qw2[:], T.pw2[:], q, p, True, True).then_inc(S["m_y%d" % k], 1)
-
-    t.wait_ge(S.k_a, 1)
-    t.wait_ge(S.k_b1, 1)
-    layer("a", "b1", "g1", "P0", 2 * NC)
-    t.wait_ge(S.k_w1, 1)
-    t.wait_ge(S.k_x, 1)
-    layer("w1", "x", "h", "P1", NC)
-    t.wait_ge(S.k_b2, 1)
-    t.wait_ge(S.act_g1, 4)
-    layer("a", "b2", "g2", "P0", 2 * NC)
-    t.wait_ge(S.k_s, 4)
+    layer("a", "bf", "gf")
+    layer("w1", "x", "h")
+    t.wait_ge(S.act_gf, 4)
+    layer("a", "bn", "gn")
     t.wait_ge(S.act_h, 4)
-    t.wait_ge(S.k_g2, 1)
-    unpack(cols("qo", own), cols("po", own), True, False)
-    t.wait_ge(S.k_w2, 1)
-    t.wait_ge(S.act_g2, 4)
-    t.wait_ge(S.k_h, 1)
-    yblock(near.index(rank), cols("qo", oh), cols("po", oh))
-    every = len(engines(topo, core, T.cores[nb]))
-    off = len(engines(topo, helpers[0], T.cores[far[0]]))
-    t.wait_ge(S.an, 2 * every)
-    yblock(near.index(nb), cols("qn", nh), cols("pn", nh))
-    unpack(cols("qn", ng), cols("pn", ng), False, False)
-    for k in (0, 1):
-        t.wait_ge(S["ag%d" % k], 2 * off)
-        unpack(T["qlg%d" % k][:], T["plg%d" % k][:], False, k == 1)
-    for k in (0, 1):
-        t.wait_ge(S["ah%d" % k], 2 * off)
-        yblock(2 + k, T["qlh%d" % k][:], T["plh%d" % k][:])
+    layer("a", "bo", "go")
 
-    act_s("g1", "P0", "tg1", 2 * NC)
-    act_s("h", "P1", "th", NC)
-    act_s("g2", "P0", "tg2", 2 * NC)
+    D = {"own": ("k_go", 1, "go", 0), "nb": ("an", 2 * len(e_nb), "n", 1), "0": ("ag0", 2 * off, "lg0", 0), "1": ("ag1", 2 * off, "lg1", 0)}
+    Y = {"own": ("k_h", 1, "o", 0, near.index(rank)), "nb": ("an", 2 * len(e_nb), "n", 0, near.index(nb)),
+         "0": ("ah0", 2 * off, "lh0", 0, 2), "1": ("ah1", 2 * off, "lh1", 0, 3)}
+    sums = [o for o in CFG["ten"] if o[0] == "d"]
+    prods = [o for o in CFG["ten"] if o[0] == "y"]
+    for o in CFG["ten"]:
+        kind, who = o.split()
+        if o == sums[0]:
+            t.wait_ge(S.act_gn, 4)
+            t.wait_ge(S.k_s, 2)
+            t.wait_ge(S.k_gift, 1)
+            t.wait_ge(S["as"], 2 * len(e_nb) + 4 * off)
+        if o == prods[0]:
+            need("w2", 0)
+            t.wait_ge(S.act_go, 4)
+        if kind == "d":
+            sem, n, buf, i = D[who]
+            t.wait_ge(S[sem], n)
+            for b in range(4):
+                ins = t.matmul_mx(T.P0[:, 512 * b:512 * b + NC], cols("qs", b), cols("ps", b), cols("q" + buf, i), cols("p" + buf, i),
+                                  o == sums[0], o == sums[-1])
+                if o == sums[-1]:
+                    ins.then_inc(S["m_z%d" % b], 1)
+        else:
+            sem, n, buf, i, k = Y[who]
+            t.wait_ge(S[sem], n)
+            t.matmul_mx(T.P1[:, 512 * k:512 * k + NC], T.qw2[:], T.pw2[:], cols("q" + buf, i), cols("p" + buf, i),
+                        True, True).then_inc(S["m_y%d" % k], 1)
 
-    def out_s(sem, dst, src, done):
-        s.wait_ge(sem, 1)
-        s.activation(dst, src, COPY).then_inc(done, 1)
+    def out(q, sem, dst, src, done):
+        q.wait_ge(sem, 1)
+        (q.activation(dst, src, COPY) if q is s else q.tensor_copy(dst, src)).then_inc(done, 1)
 
-    def out_v(sem, dst, src, done):
-        v.wait_ge(sem, 1)
-        v.tensor_copy(dst, src).then_inc(done, 1)
+    def out_y(first, buf, at, done):
+        for k in (0, 1):
+            j = first + k
+            out((v, s)[k], S["m_y%d" % j], T[buf][:, k * NC:(k + 1) * NC], T.P1[:, 512 * j:512 * j + NC], done)
+        y.wait_ge(done, 2)
+        y.dma_start(T.y[:, at * NC:(at + 2) * NC], T[buf][:]).then_inc(S.stored, 16)
 
-    out_v(S.m_y0, T.yt1[:, 0:NC], T.P0[:, 0:NC], S.cy1)
-    out_s(S.m_y1, T.yt1[:, NC:2 * NC], T.P0[:, 512:512 + NC], S.cy1)
-    for b in range(4):
-        (out_s if b % 2 == 0 else out_v)(S["m_z%d" % b], T.zt[:, b:W:4], T.P1[:, 512 * b:512 * b + NC], S.cz)
-    out_v(S.m_y2, T.yt2[:, 0:NC], T.P0[:, 1024:1024 + NC], S.cy2)
-    out_s(S.m_y3, T.yt2[:, NC:2 * NC], T.P0[:, 1536:1536 + NC], S.cy2)
-
-    y.wait_ge(S.cy1, 2)
-    y.dma_start(T.y[:, n0 * NC:(n0 + 2) * NC], T.yt1[:]).then_inc(S.stored, 16)
-    y.wait_ge(S.cz, 4)
-    y.dma_start(T.z[:], T.zt[:]).then_inc(S.stored, 16)
-    y.wait_ge(S.cy2, 2)
-    y.dma_start(T.y[:, f0 * NC:(f0 + 2) * NC], T.yt2[:]).then_inc(S.stored, 16)
+    for o in CFG["ten"]:
+        if o == sums[-1]:
+            for b in range(4):
+                out((s, v)[b % 2], S["m_z%d" % b], T.zt[:, b:W:4], T.P0[:, 512 * b:512 * b + NC], S.cz)
+            y.wait_ge(S.cz, 4)
+            y.dma_start(T.z[:], T.zt[:]).then_inc(S.stored, 16)
+        elif o == "y nb":
+            out_y(0, "yt1", near[0], S.cy1)
+        elif o == "y 1":
+            out_y(2, "yt2", far[0], S.cy2)
     y.wait_ge(S.stored, 48)
-
-    g.wait_ge(S.ones, 1)
-    g.affine_select(T.eye[:], T.ones[:], [[-1, W + 4]], AluOpType.is_equal, 0.0, 3, 4).then_inc(S.eye, 1)
 
     def to_relays(srcs, dst, sem):
         tr = []
@@ -247,15 +272,16 @@ def rank_core(g, core, rank, T, topo, P, R):
                                         remote_sem=sem, src=srcs[k], dst=dst))
         g.remote_dma_fused(tr, local_sem=S.sent)
 
-    g.wait_ge(S.k_g1, 1)
-    to_relays([u8(cols("qg1", k)) for k in (0, 1)], u8(T.qrg[:]), S.rgc)
-    to_relays([cols("pg1", k) for k in (0, 1)], T.prg[:], S.rgp)
+    g.wait_ge(S.k_gift, 1)
+    send(g, topo, T.cores[nb], sum(e_nb), T.qs, T.ps, gift * NC, gift * NC + NC // 2, S["as"], S["as"], S.sent)
+    g.wait_ge(S.k_gf, 1)
+    to_relays([u8(cols("qgf", k)) for k in (0, 1)], u8(T.qrg[:]), S.rgc)
+    to_relays([cols("pgf", k) for k in (0, 1)], T.prg[:], S.rgp)
     g.wait_ge(S.k_h, 1)
-    to_relays([u8(cols("qo", oh))] * 2, u8(T.qrh[:]), S.rhc)
-    to_relays([cols("po", oh)] * 2, T.prh[:], S.rhp)
+    to_relays([u8(cols("qo", 0))] * 2, u8(T.qrh[:]), S.rhc)
+    to_relays([cols("po", 0)] * 2, T.prh[:], S.rhp)
     rid, pid, _ = topo.addr(T.cores[nb])
-    e = engines(topo, core, T.cores[nb])
-    g.wait_ge(S.k_g2, 1)
-    g.remote_dma(u8(T.qn[:]), u8(cols("qo", send, 2)), S.an, S.sent, pid, rid, sum(e))
-    g.remote_dma(T.pn[:], cols("po", send, 2), S.an, S.sent, pid, rid, sum(e))
-    g.wait_ge(S.sent, 6 * len(e))
+    g.wait_ge(S.k_gn, 1)
+    g.remote_dma(u8(T.qn[:]), u8(T.qo[:]), S.an, S.sent, pid, rid, sum(e_nb))
+    g.remote_dma(T.pn[:], T.po[:], S.an, S.sent, pid, rid, sum(e_nb))
+    g.wait_ge(S.sent, 8 * len(e_nb))

@@ -6,57 +6,61 @@ W = 4 * NC
 FACTOR = 0.029
 
 CFG = {
-    "sync": [("a", 0, 2), ("x", 0, 1), ("w1", 2, 2), ("l_a0", 16), ("bn", 0, 1), ("bo", 0, 1), ("w2", 0, 1)],
-    "scalar": [("bf", 0, 2), ("a", 2, 2), ("w1", 0, 2)],
-    "vec": [("s", "gift"), ("q", "bf", 0), ("q", "a", 0), ("q", "a", 2), ("q", "x", 0), ("q", "w1", 0), ("t", "gf"),
-            ("q", "w1", 2), ("r", "h", 2), ("t", "h"), ("q", "bn", 0), ("r", "gn", 1), ("r", "gn", 3), ("t", "gn"),
-            ("q", "bo", 0), ("s", "rest"), ("r", "go", 1), ("r", "go", 3), ("t", "go"), ("q", "w2", 0)],
-    "sca": [("r", "gf", 0), ("r", "gf", 1), ("r", "gf", 2), ("r", "gf", 3), ("r", "h", 0), ("r", "h", 1), ("r", "h", 3),
-            ("r", "gn", 0), ("r", "gn", 2), ("r", "go", 0), ("r", "go", 2)],
-    "ten": ["d own", "y own", "d nb", "y nb", "d 0", "d 1", "y 0", "y 1"],
+    "sync": [("a", 0, 1), ("a", 2, 1), ("bf", 1, 1), ("w1", 0, 1), ("w1", 2, 1), ("bp", 0, 1), ("w2", 0, 1), ("bp", 1, 1)],
+    "scalar": [("a", 1, 1), ("bf", 0, 1), ("a", 3, 1), ("x", 0, 1), ("w1", 1, 1), ("w1", 3, 1)],
+    "vec": [("s", "gift"), ("s", 1), ("q", "a", 1, 1), ("s", 0), ("q", "bf", 0, 1), ("q", "a", 0, 1), ("q", "a", 2, 1),
+            ("q", "a", 3, 1), ("r", "g0", 0), ("q", "bf", 1, 1), ("q", "x", 0, 1), ("t", "g0"), ("q", "w1", 0, 2),
+            ("q", "w1", 2, 1), ("r", "g1", 3), ("t", "g1"), ("q", "w1", 3, 1), ("q", "bp", 0, 1), ("r", "h", 3), ("t", "h"),
+            ("q", "bp", 1, 1), ("r", "gn", 1), ("r", "gn", 3), ("t", "gn"), ("t", "go"), ("q", "w2", 0, 1)],
+    "sca": [("r", "g0", 1), ("r", "g0", 2), ("r", "g0", 3), ("r", "g1", 0), ("r", "g1", 2), ("r", "g1", 1), ("r", "h", 0),
+            ("r", "h", 2), ("r", "h", 1), ("r", "gn", 0), ("r", "gn", 2), ("r", "go", 0), ("r", "go", 2), ("r", "go", 3),
+            ("r", "go", 1)],
+    "ten": ["L g0", "L g1", "L h", "L gn", "L go", "d own", "y own", "d nb", "y nb", "d 0", "d 1", "y 0", "y 1"],
+    "gp": ["giftp", "g0c", "g0p", "g1c", "g1p", "hc", "hp", "giftc", "nbc", "nbp"],
+    "route": {"g0c": (0, [0]), "g0p": (1, [0]), "g1c": (1, [1]), "g1p": (0, [1]), "hc": (0, [0, 1]), "hp": (1, [0, 1])},
+    "ystore": [["own", "nb"], ["0"], ["1"]],
+    "banks": {"g0": "P0", "g1": "P1", "h": "P0", "gn": "P1", "go": "P0", "z": "P1", "y": "P0"},
 }
-TILES = {"a": 4, "bf": 2, "bn": 1, "bo": 1, "w1": 4, "x": 1, "w2": 1}
-MADE = {"gf": (2, "P0"), "gn": (1, "P0"), "go": (1, "P1"), "h": (1, "P1")}
+RELAYS = 2
+TILES = {"a": 4, "bf": 2, "bp": 2, "w1": 4, "x": 1, "w2": 1}
+LAYERS = {"g0": ("a", "bf"), "g1": ("a", "bf"), "gn": ("a", "bp"), "go": ("a", "bp"), "h": ("w1", "x")}
+ITEMS = ("g0", "g1", "h")
+WHERE = {"g0": ("g", 0), "g1": ("g", 1), "gn": ("o", 1), "go": ("go", 0), "h": ("o", 0)}
 
 SCRATCH = {
-    "ones": ("sbuf", [128, W + 4], "bfloat16"),
+    "ones": ("sbuf", [32, NC], "bfloat16"),
+    "blk": ("sbuf", [32, NC], "bfloat16"),
     "eye": ("sbuf", [128, W + 4], "bfloat16"),
     "zt": ("sbuf", [128, W], "float32"),
-    "yt1": ("sbuf", [128, 2 * NC], "float32"),
-    "yt2": ("sbuf", [128, 2 * NC], "float32"),
+    "yt": ("sbuf", [128, 4 * NC], "float32"),
     "P0": ("psum", [128, 2048], "float32"),
     "P1": ("psum", [128, 2048], "float32"),
 }
 for _n in TILES:
     SCRATCH["t" + _n] = ("sbuf", [128, TILES[_n] * W], "bfloat16")
-for _n in MADE:
-    SCRATCH["t" + _n] = ("sbuf", [128, MADE[_n][0] * W], "bfloat16")
-for _n, _w in (("a", 4), ("bf", 2), ("bn", 1), ("bo", 1), ("w1", 4), ("x", 1), ("w2", 1), ("s", 4),
-               ("gf", 2),
+for _n in LAYERS:
+    SCRATCH["t" + _n] = ("sbuf", [128, W], "bfloat16")
+for _n, _w in (("a", 4), ("bf", 2), ("bp", 2), ("w1", 4), ("x", 1), ("w2", 1), ("s", 4),
+               ("g", 2),
                ("o", 2),
                ("go", 1),
                ("n", 2),
-               ("lg0", 1), ("lg1", 1), ("lh0", 1), ("lh1", 1),
-               ("rg", 1), ("rh", 1)):
+               ("l", 4),
+               ("r", 3)):
     SCRATCH["q" + _n] = ("sbuf", [128, _w * NC], "float8_e4m3fn_x4")
     SCRATCH["p" + _n] = ("sbuf", [128, _w * NC], "uint8")
 
 SEMAPHORES = (["l_%s%d" % (n, i) for n in TILES for i in range(TILES[n])]
               + ["k_%s%d" % (n, i) for n in TILES for i in range(TILES[n])]
-              + ["k_s", "k_gift"] + ["k_" + n for n in MADE] + ["act_" + n for n in MADE]
-              + ["ones", "eye", "cy1", "cy2", "cz", "stored", "sent"]
-              + ["m_%s%d" % (n, b) for n in list(MADE) + ["z", "y"] for b in range(4)]
-              + ["as", "an", "ag0", "ag1", "ah0", "ah1", "rgc", "rgp", "rhc", "rhp"])
+              + ["k_s", "k_gift"] + ["k_" + n for n in LAYERS] + ["act_" + n for n in LAYERS]
+              + ["ones", "zero", "blk", "eye", "cz", "stored", "sent"] + ["cy%d" % i for i in range(4)]
+              + ["m_%s%d" % (n, b) for n in list(LAYERS) + ["z", "y"] for b in range(4)]
+              + ["as", "an", "ag0", "ag1", "ah0", "ah1"] + ["r_%s%s" % (n, c) for n in ITEMS for c in "cp"])
 
 
 def engines(topo, src, dst):
     m = topo.mask(src, dst)
     return [1 << i for i in range(m.bit_length()) if (m >> i) & 1]
-
-
-def dest(topo, c):
-    rid, pid, _ = topo.addr(c)
-    return DstId(rid=rid, pnc=pid)
 
 
 def plan(T, topo):
@@ -67,10 +71,12 @@ def plan(T, topo):
         c = cores[r]
         near = [s for s in ranks if topo.chip(cores[s]) == topo.chip(c)]
         far = [s for s in ranks if s not in near]
-        found = [k for k in range(max(c - 16, 0), c + 16) if topo.chip(k) == topo.chip(c) and topo.die(k) == topo.die(c)
-                 and k not in cores and all(topo.may_write(k, cores[f]) for f in far)]
-        P.append({"near": near, "far": far, "nb": [s for s in near if s != r][0], "lack": 3 if r == near[0] else 0,
-                  "relays": found[:len(far)]})
+        turn = near.index(r)
+        far = far[turn:] + far[:turn]
+        relays = [k for k in range(max(c - 16, 0), c + 16) if topo.chip(k) == topo.chip(c) and topo.die(k) == topo.die(c)
+                  and k not in cores and all(topo.may_write(k, cores[f]) for f in far)]
+        P.append({"near": near, "far": far, "nb": [s for s in near if s != r][0], "relays": relays[:RELAYS],
+                  "lack": 3 if r == near[0] else 0})
     return P
 
 
@@ -85,203 +91,205 @@ def rank_program(g, core, T, topo):
             relay_core(g, core, r, P[r]["relays"].index(core), T, topo, P)
 
 
-def u8(ap):
-    return ap.bitcast(dt.uint8)
+def part(T, c, buf, at, n=NC):
+    if c == "c":
+        return T["q" + buf][:, at:at + n].bitcast(dt.uint8)
+    return T["p" + buf][:, at:at + n]
 
 
 def make_eye(g, T):
-    g.vector.memset(T.ones[:], 1.0).then_inc(T.sem.ones, 1)
-    g.wait_ge(T.sem.ones, 1)
-    g.affine_select(T.eye[:], T.ones[:], [[-1, W + 4]], AluOpType.is_equal, 0.0, 3, 4).then_inc(T.sem.eye, 1)
+    v, S = g.vector, T.sem
+    v.memset(T.ones[:], 1.0).then_inc(S.ones, 1)
+    v.memset(T.eye[:], 0.0).then_inc(S.zero, 1)
+    g.wait_ge(S.ones, 1)
+    g.affine_select(T.blk[:], T.ones[:], [[-1, NC]], AluOpType.is_equal, 0.0, 3, 4).then_inc(S.blk, 1)
+    v.wait_ge(S.zero, 1)
+    v.wait_ge(S.blk, 1)
+    for i in range(4):
+        v.tensor_copy(T.eye[32 * i:32 * i + 32, NC * i:NC * i + NC], T.blk[:]).then_inc(S.eye, 1)
+    v.wait_ge(S.eye, 4)
 
 
 def quant_s(g, T, b, sem):
     g.vector.quantize_mx(T.qs[:, b * NC:(b + 1) * NC], T.ps[:, b * NC:(b + 1) * NC], T.eye[:, 3 - b:3 - b + W]).then_inc(sem, 1)
 
 
-def send(g, topo, to, mask, codes, planes, a, b, sem_c, sem_p, sent):
-    rid, pid, _ = topo.addr(to)
-    g.remote_dma(u8(codes[:, a:b]), u8(codes[:, a:b]), sem_c, sent, pid, rid, mask)
-    g.remote_dma(planes[:, a:b], planes[:, a:b], sem_p, sent, pid, rid, mask)
-
-
 def relay_core(g, core, r, k, T, topo, P):
-    S = T.sem
-    d = P[r]["far"][k]
-    to, home, lack = T.cores[d], T.cores[r], P[r]["lack"]
-    me = P[d]["far"].index(r)
-    eng = engines(topo, core, to)
+    S, cores, far, lack = T.sem, T.cores, P[r]["far"], P[r]["lack"]
+    eng = engines(topo, core, cores[far[0]])
     mask, n = sum(eng), len(eng)
     make_eye(g, T)
-    g.vector.wait_ge(S.eye, 1)
     quant_s(g, T, lack, S.k_s)
     g.wait_ge(S.k_s, 1)
-    c = lack * NC + NC // 2 + k * (NC // 4)
-    send(g, topo, home, mask, T.qs, T.ps, c, c + NC // 4, S["as"], S["as"], S.sent)
-    rid, pid, _ = topo.addr(to)
-    half = len(engines(topo, home, core)) // 2
-    for t in ("g", "h"):
-        arrive = S["a%s%d" % (t, me)]
-        g.wait_ge(S["r%sc" % t], half)
-        g.remote_dma(u8(T["ql%s%d" % (t, me)][:, 0:NC]), u8(T["qr" + t][:, 0:NC]), arrive, S.sent, pid, rid, mask)
-        g.wait_ge(S["r%sp" % t], half)
-        g.remote_dma(T["pl%s%d" % (t, me)][:, 0:NC], T["pr" + t][:, 0:NC], arrive, S.sent, pid, rid, mask)
-    g.wait_ge(S.sent, 6 * n)
+    w = NC // 2 // RELAYS
+    a = lack * NC + NC // 2 + k * w
+    rid, pid, _ = topo.addr(cores[r])
+    for c in "cp":
+        g.remote_dma(part(T, c, "s", a, w), part(T, c, "s", a, w), S["as"], S.sent, pid, rid, mask)
+    cnt = 2
+    for o in CFG["gp"]:
+        if o not in CFG["route"] or CFG["route"][o][0] != k:
+            continue
+        i, c = o[:-1], o[-1]
+        g.wait_ge(S["r_" + o], len(engines(topo, cores[r], core)))
+        for f in CFG["route"][o][1]:
+            d = far[f]
+            me = P[d]["far"].index(r)
+            rid, pid, _ = topo.addr(cores[d])
+            g.remote_dma(part(T, c, "l", (me + (2 if i == "h" else 0)) * NC), part(T, c, "r", ITEMS.index(i) * NC),
+                         S["a%s%d" % (i[0], me)], S.sent, pid, rid, mask)
+            cnt += 1
+    g.wait_ge(S.sent, cnt * n)
 
 
 def rank_core(g, core, rank, T, topo, P):
     S = T.sem
-    near, far, nb, lack, helpers = [P[rank][k] for k in ("near", "far", "nb", "lack", "relays")]
+    near, far, nb, helpers, lack = [P[rank][k] for k in ("near", "far", "nb", "relays", "lack")]
     gift = P[nb]["lack"]
     v, s, t, y = g.vector, g.scalar, g.tensor, g.sync
     RELU, COPY = ActivationFunctionType.Relu, ActivationFunctionType.Copy
     e_nb = engines(topo, core, T.cores[nb])
     off = len(engines(topo, helpers[0], T.cores[far[0]]))
+    bank = CFG["banks"]
 
     def cols(buf, i, n=1):
         return T[buf][:, i * NC:(i + n) * NC]
 
-    where = {"gf": ("gf", 0), "gn": ("o", 1), "go": ("go", 0), "h": ("o", 0)}
-    source = {"a": (T.a, 0), "bf": (T.b, far[0]), "bn": (T.b, nb), "bo": (T.b, rank), "w1": (T.w1, 0), "x": (T.x, 0), "w2": (T.w2, 0)}
-    parts = [p for p in CFG["sync"] + CFG["scalar"] if len(p) == 3]
-    size = {(n, i): k for n, i, k in parts}
+    every = list(range(4))
+    source = {"a": (T.a, every), "bf": (T.b, far), "bp": (T.b, [nb, rank]), "w1": (T.w1, every), "x": (T.x, [0]), "w2": (T.w2, [0])}
+    loads = CFG["sync"] + CFG["scalar"]
+    quants = [o[1:] for o in CFG["vec"] if o[0] == "q"]
+    tile = {"g0": 0, "g1": 1, "gn": 0, "go": 1, "h": 0}
 
-    def piece(n, tile):
-        return [(m, i) for m, i, k in parts if m == n and i <= tile < i + k][0]
+    def piece(n, tile, pieces):
+        return [(m, i) for m, i, k in pieces if m == n and i <= tile < i + k][0]
 
     def load(q, queue):
-        for p in queue:
-            if len(p) == 2:
-                q.wait_ge(S[p[0]], p[1])
-                continue
-            n, i, k = p
+        for n, i, k in queue:
             src, at = source[n]
-            q.dma_start(T["t" + n][:, i * W:(i + k) * W], src[:, (at + i) * W:(at + i + k) * W]).then_inc(S["l_%s%d" % (n, i)], 16)
+            q.dma_start(T["t" + n][:, i * W:(i + k) * W], src[:, at[i] * W:(at[i] + k) * W]).then_inc(S["l_%s%d" % (n, i)], 16)
 
     load(y, CFG["sync"])
     load(s, CFG["scalar"])
     make_eye(g, T)
 
     def result(q, n, b):
-        k, bank = MADE[n]
         q.wait_ge(S["m_%s%d" % (n, b)], 1)
-        dst, src = T["t" + n][:, b:k * W:4], T[bank][:, 512 * b:512 * b + k * NC]
+        dst, src = T["t" + n][:, b:W:4], T[bank[n]][:, 512 * b:512 * b + NC]
         i = q.activation(dst, src, RELU, scale=FACTOR) if q is s else q.tensor_scalar(dst, src, 0.0, FACTOR, AluOpType.max, AluOpType.mult)
         i.then_inc(S["act_" + n], 1)
 
+    rest = [b for b in range(4) if b not in (lack, gift)]
     for op in CFG["vec"]:
         n = op[1]
         if op[0] == "s":
-            v.wait_ge(S.eye, 1)
             if n == "gift":
                 quant_s(g, T, gift, S.k_gift)
             else:
-                for b in range(4):
-                    if b not in (gift, lack):
-                        quant_s(g, T, b, S.k_s)
+                quant_s(g, T, rest[n], S.k_s)
         elif op[0] == "q":
-            i = op[2]
-            k = size[n, i]
-            v.wait_ge(S["l_%s%d" % (n, i)], 16)
+            i, k = op[2:]
+            for l in sorted({piece(n, j, loads) for j in range(i, i + k)}):
+                v.wait_ge(S["l_%s%d" % l], 16)
             v.quantize_mx(cols("q" + n, i, k), cols("p" + n, i, k), T["t" + n][:, i * W:(i + k) * W]).then_inc(S["k_%s%d" % (n, i)], 1)
         elif op[0] == "r":
             result(v, n, op[2])
         else:
-            buf, i = where[n]
+            buf, i = WHERE[n]
             v.wait_ge(S["act_" + n], 4)
-            v.quantize_mx(cols("q" + buf, i, MADE[n][0]), cols("p" + buf, i, MADE[n][0]), T["t" + n][:]).then_inc(S["k_" + n], 1)
+            v.quantize_mx(cols("q" + buf, i), cols("p" + buf, i), T["t" + n][:]).then_inc(S["k_" + n], 1)
     for op in CFG["sca"]:
         result(s, op[1], op[2])
 
     def need(n, tile):
-        t.wait_ge(S["k_%s%d" % piece(n, tile)], 1)
+        t.wait_ge(S["k_%s%d" % piece(n, tile, quants)], 1)
 
-    def layer(w, m, n):
-        width, bank = MADE[n][0] * NC, MADE[n][1]
-        need(m, 0)
-        for b in range(4):
-            need(w, b)
-            t.matmul_mx(T[bank][:, 512 * b:512 * b + width], cols("q" + w, b), cols("p" + w, b), T["q" + m][:], T["p" + m][:],
-                        True, True).then_inc(S["m_%s%d" % (n, b)], 1)
+    taken = {}
 
-    layer("a", "bf", "gf")
-    layer("w1", "x", "h")
-    t.wait_ge(S.act_gf, 4)
-    layer("a", "bn", "gn")
-    t.wait_ge(S.act_h, 4)
-    layer("a", "bo", "go")
+    def free(b):
+        if b in taken:
+            t.wait_ge(S["act_" + taken[b]], 4)
 
-    D = {"own": ("k_go", 1, "go", 0), "nb": ("an", 2 * len(e_nb), "n", 1), "0": ("ag0", 2 * off, "lg0", 0), "1": ("ag1", 2 * off, "lg1", 0)}
-    Y = {"own": ("k_h", 1, "o", 0, near.index(rank)), "nb": ("an", 2 * len(e_nb), "n", 0, near.index(nb)),
-         "0": ("ah0", 2 * off, "lh0", 0, 2), "1": ("ah1", 2 * off, "lh1", 0, 3)}
+    D = {"own": ("k_go", 1, "go", 0), "nb": ("an", 2 * len(e_nb), "n", 1), "0": ("ag0", 2 * off, "l", 0), "1": ("ag1", 2 * off, "l", 1)}
+    Y = {"own": ("k_h", 1, "o", 0), "nb": ("an", 2 * len(e_nb), "n", 0), "0": ("ah0", 2 * off, "l", 2), "1": ("ah1", 2 * off, "l", 3)}
+    block = {"own": rank, "nb": nb, "0": far[0], "1": far[1]}
     sums = [o for o in CFG["ten"] if o[0] == "d"]
     prods = [o for o in CFG["ten"] if o[0] == "y"]
     for o in CFG["ten"]:
         kind, who = o.split()
-        if o == sums[0]:
-            t.wait_ge(S.act_gn, 4)
-            t.wait_ge(S.k_s, 2)
-            t.wait_ge(S.k_gift, 1)
-            t.wait_ge(S["as"], 2 * len(e_nb) + 4 * off)
-        if o == prods[0]:
-            need("w2", 0)
-            t.wait_ge(S.act_go, 4)
-        if kind == "d":
+        if kind == "L":
+            w, m = LAYERS[who]
+            i = tile[who]
+            free(bank[who])
+            taken[bank[who]] = who
+            need(m, i)
+            for b in range(4):
+                need(w, b)
+                t.matmul_mx(T[bank[who]][:, 512 * b:512 * b + NC], cols("q" + w, b), cols("p" + w, b), cols("q" + m, i), cols("p" + m, i),
+                            True, True).then_inc(S["m_%s%d" % (who, b)], 1)
+        elif kind == "d":
+            if o == sums[0]:
+                free(bank["z"])
+                t.wait_ge(S.k_s, 2)
+                t.wait_ge(S.k_gift, 1)
+                t.wait_ge(S["as"], 2 * len(e_nb) + 2 * RELAYS * off)
             sem, n, buf, i = D[who]
             t.wait_ge(S[sem], n)
             for b in range(4):
-                ins = t.matmul_mx(T.P0[:, 512 * b:512 * b + NC], cols("qs", b), cols("ps", b), cols("q" + buf, i), cols("p" + buf, i),
+                ins = t.matmul_mx(T[bank["z"]][:, 512 * b:512 * b + NC], cols("qs", b), cols("ps", b), cols("q" + buf, i), cols("p" + buf, i),
                                   o == sums[0], o == sums[-1])
                 if o == sums[-1]:
                     ins.then_inc(S["m_z%d" % b], 1)
         else:
-            sem, n, buf, i, k = Y[who]
+            if o == prods[0]:
+                need("w2", 0)
+                free(bank["y"])
+            sem, n, buf, i = Y[who]
+            k = block[who]
             t.wait_ge(S[sem], n)
-            t.matmul_mx(T.P1[:, 512 * k:512 * k + NC], T.qw2[:], T.pw2[:], cols("q" + buf, i), cols("p" + buf, i),
+            t.matmul_mx(T[bank["y"]][:, 512 * k:512 * k + NC], T.qw2[:], T.pw2[:], cols("q" + buf, i), cols("p" + buf, i),
                         True, True).then_inc(S["m_y%d" % k], 1)
 
     def out(q, sem, dst, src, done):
         q.wait_ge(sem, 1)
         (q.activation(dst, src, COPY) if q is s else q.tensor_copy(dst, src)).then_inc(done, 1)
 
-    def out_y(first, buf, at, done):
-        for k in (0, 1):
-            j = first + k
-            out((v, s)[k], S["m_y%d" % j], T[buf][:, k * NC:(k + 1) * NC], T.P1[:, 512 * j:512 * j + NC], done)
-        y.wait_ge(done, 2)
-        y.dma_start(T.y[:, at * NC:(at + 2) * NC], T[buf][:]).then_inc(S.stored, 16)
-
+    n_st, turn = 0, 0
     for o in CFG["ten"]:
+        kind, who = o.split()
         if o == sums[-1]:
             for b in range(4):
-                out((s, v)[b % 2], S["m_z%d" % b], T.zt[:, b:W:4], T.P0[:, 512 * b:512 * b + NC], S.cz)
+                out((s, v)[b % 2], S["m_z%d" % b], T.zt[:, b:W:4], T[bank["z"]][:, 512 * b:512 * b + NC], S.cz)
             y.wait_ge(S.cz, 4)
             y.dma_start(T.z[:], T.zt[:]).then_inc(S.stored, 16)
-        elif o == "y nb":
-            out_y(0, "yt1", near[0], S.cy1)
-        elif o == "y 1":
-            out_y(2, "yt2", far[0], S.cy2)
-    y.wait_ge(S.stored, 48)
+            n_st += 1
+        elif kind == "y":
+            j, grp = [(j, grp) for j, grp in enumerate(CFG["ystore"]) if who in grp][0]
+            k = block[who]
+            out((v, s)[turn % 2], S["m_y%d" % k], cols("yt", k), T[bank["y"]][:, 512 * k:512 * k + NC], S["cy%d" % j])
+            turn += 1
+            if who == [p.split()[1] for p in prods if p.split()[1] in grp][-1]:
+                a = min(block[w] for w in grp)
+                y.wait_ge(S["cy%d" % j], len(grp))
+                y.dma_start(T.y[:, a * NC:(a + len(grp)) * NC], cols("yt", a, len(grp))).then_inc(S.stored, 16)
+                n_st += 1
+    y.wait_ge(S.stored, 16 * n_st)
 
-    def to_relays(srcs, dst, sem):
-        tr = []
-        for k in (0, 1):
-            e = engines(topo, core, helpers[k])
-            h = len(e) // 2
-            tr.append(RemoteDMATransfer(dst_ids=[dest(topo, helpers[k])], dma_engine_mask=sum(e[k * h:(k + 1) * h]),
-                                        remote_sem=sem, src=srcs[k], dst=dst))
-        g.remote_dma_fused(tr, local_sem=S.sent)
-
-    g.wait_ge(S.k_gift, 1)
-    send(g, topo, T.cores[nb], sum(e_nb), T.qs, T.ps, gift * NC, gift * NC + NC // 2, S["as"], S["as"], S.sent)
-    g.wait_ge(S.k_gf, 1)
-    to_relays([u8(cols("qgf", k)) for k in (0, 1)], u8(T.qrg[:]), S.rgc)
-    to_relays([cols("pgf", k) for k in (0, 1)], T.prg[:], S.rgp)
-    g.wait_ge(S.k_h, 1)
-    to_relays([u8(cols("qo", 0))] * 2, u8(T.qrh[:]), S.rhc)
-    to_relays([cols("po", 0)] * 2, T.prh[:], S.rhp)
-    rid, pid, _ = topo.addr(T.cores[nb])
-    g.wait_ge(S.k_gn, 1)
-    g.remote_dma(u8(T.qn[:]), u8(T.qo[:]), S.an, S.sent, pid, rid, sum(e_nb))
-    g.remote_dma(T.pn[:], T.po[:], S.an, S.sent, pid, rid, sum(e_nb))
-    g.wait_ge(S.sent, 8 * len(e_nb))
+    for o in CFG["gp"]:
+        i, c = o[:-1], o[-1]
+        if o in CFG["route"]:
+            to = helpers[CFG["route"][o][0]]
+            done, arrive = ["k_" + i], "r_" + o
+            buf, at = WHERE[i]
+            src, dst = part(T, c, buf, at * NC), part(T, c, "r", ITEMS.index(i) * NC)
+        elif i == "gift":
+            to, done, arrive = T.cores[nb], ["k_gift"], "as"
+            src = dst = part(T, c, "s", gift * NC, NC // 2)
+        else:
+            to, done, arrive = T.cores[nb], ["k_h", "k_gn"], "an"
+            src, dst = part(T, c, "o", 0, 2 * NC), part(T, c, "n", 0, 2 * NC)
+        for d in done:
+            g.wait_ge(S[d], 1)
+        rid, pid, _ = topo.addr(to)
+        g.remote_dma(dst, src, S[arrive], S.sent, pid, rid, sum(engines(topo, core, to)))
+    g.wait_ge(S.sent, len(CFG["gp"]) * len(e_nb))

from concourse.bass import DstId, RemoteDMATransfer
from concourse.mybir import dt, AluOpType, ActivationFunctionType

NC = 128
W = 4 * NC
FACTOR = 0.029

CFG = {
    "sync": [("a", 0, 1), ("a", 2, 1), ("bf", 1, 1), ("w1", 0, 1), ("w1", 2, 1), ("bp", 0, 1), ("w2", 0, 1), ("bp", 1, 1)],
    "scalar": [("a", 1, 1), ("bf", 0, 1), ("a", 3, 1), ("x", 0, 1), ("w1", 1, 1), ("w1", 3, 1)],
    "vec": [("s", "gift"), ("s", 1), ("q", "a", 1, 1), ("s", 0), ("q", "bf", 0, 1), ("q", "a", 0, 1), ("q", "a", 2, 1),
            ("q", "a", 3, 1), ("r", "g0", 0), ("q", "bf", 1, 1), ("q", "x", 0, 1), ("t", "g0"), ("q", "w1", 0, 2),
            ("q", "w1", 2, 1), ("r", "g1", 3), ("t", "g1"), ("q", "w1", 3, 1), ("q", "bp", 0, 1), ("r", "h", 3), ("t", "h"),
            ("q", "bp", 1, 1), ("r", "gn", 1), ("r", "gn", 3), ("t", "gn"), ("t", "go"), ("q", "w2", 0, 1)],
    "sca": [("r", "g0", 1), ("r", "g0", 2), ("r", "g0", 3), ("r", "g1", 0), ("r", "g1", 2), ("r", "g1", 1), ("r", "h", 0),
            ("r", "h", 2), ("r", "h", 1), ("r", "gn", 0), ("r", "gn", 2), ("r", "go", 0), ("r", "go", 2), ("r", "go", 3),
            ("r", "go", 1)],
    "ten": ["L g0", "L g1", "L h", "L gn", "L go", "d own", "y own", "d nb", "y nb", "d 0", "d 1", "y 0", "y 1"],
    "gp": ["giftp", "g0c", "g0p", "g1c", "g1p", "hc", "hp", "giftc", "nbc", "nbp"],
    "route": {"g0c": (0, [0]), "g0p": (1, [0]), "g1c": (1, [1]), "g1p": (0, [1]), "hc": (0, [0, 1]), "hp": (1, [0, 1])},
    "ystore": [["own", "nb"], ["0"], ["1"]],
    "banks": {"g0": "P0", "g1": "P1", "h": "P0", "gn": "P1", "go": "P0", "z": "P1", "y": "P0"},
}
RELAYS = 2
TILES = {"a": 4, "bf": 2, "bp": 2, "w1": 4, "x": 1, "w2": 1}
LAYERS = {"g0": ("a", "bf"), "g1": ("a", "bf"), "gn": ("a", "bp"), "go": ("a", "bp"), "h": ("w1", "x")}
ITEMS = ("g0", "g1", "h")
WHERE = {"g0": ("g", 0), "g1": ("g", 1), "gn": ("o", 1), "go": ("go", 0), "h": ("o", 0)}

SCRATCH = {
    "ones": ("sbuf", [32, NC], "bfloat16"),
    "blk": ("sbuf", [32, NC], "bfloat16"),
    "eye": ("sbuf", [128, W + 4], "bfloat16"),
    "zt": ("sbuf", [128, W], "float32"),
    "yt": ("sbuf", [128, 4 * NC], "float32"),
    "P0": ("psum", [128, 2048], "float32"),
    "P1": ("psum", [128, 2048], "float32"),
}
for _n in TILES:
    SCRATCH["t" + _n] = ("sbuf", [128, TILES[_n] * W], "bfloat16")
for _n in LAYERS:
    SCRATCH["t" + _n] = ("sbuf", [128, W], "bfloat16")
for _n, _w in (("a", 4), ("bf", 2), ("bp", 2), ("w1", 4), ("x", 1), ("w2", 1), ("s", 4),
               ("g", 2),
               ("o", 2),
               ("go", 1),
               ("n", 2),
               ("l", 4),
               ("r", 3)):
    SCRATCH["q" + _n] = ("sbuf", [128, _w * NC], "float8_e4m3fn_x4")
    SCRATCH["p" + _n] = ("sbuf", [128, _w * NC], "uint8")

SEMAPHORES = (["l_%s%d" % (n, i) for n in TILES for i in range(TILES[n])]
              + ["k_%s%d" % (n, i) for n in TILES for i in range(TILES[n])]
              + ["k_s", "k_gift"] + ["k_" + n for n in LAYERS] + ["act_" + n for n in LAYERS]
              + ["ones", "zero", "blk", "eye", "cz", "stored", "sent"] + ["cy%d" % i for i in range(4)]
              + ["m_%s%d" % (n, b) for n in list(LAYERS) + ["z", "y"] for b in range(4)]
              + ["as", "an", "ag0", "ag1", "ah0", "ah1"] + ["r_%s%s" % (n, c) for n in ITEMS for c in "cp"])


def engines(topo, src, dst):
    m = topo.mask(src, dst)
    return [1 << i for i in range(m.bit_length()) if (m >> i) & 1]


def plan(T, topo):
    cores = list(T.cores)
    ranks = range(len(cores))
    P = []
    for r in ranks:
        c = cores[r]
        near = [s for s in ranks if topo.chip(cores[s]) == topo.chip(c)]
        far = [s for s in ranks if s not in near]
        turn = near.index(r)
        far = far[turn:] + far[:turn]
        relays = [k for k in range(max(c - 16, 0), c + 16) if topo.chip(k) == topo.chip(c) and topo.die(k) == topo.die(c)
                  and k not in cores and all(topo.may_write(k, cores[f]) for f in far)]
        P.append({"near": near, "far": far, "nb": [s for s in near if s != r][0], "relays": relays[:RELAYS],
                  "lack": 3 if r == near[0] else 0})
    return P


def rank_program(g, core, T, topo):
    P = plan(T, topo)
    rank = T.rank_of(core)
    if rank is not None:
        rank_core(g, core, rank, T, topo, P)
        return
    for r in range(len(P)):
        if core in P[r]["relays"]:
            relay_core(g, core, r, P[r]["relays"].index(core), T, topo, P)


def part(T, c, buf, at, n=NC):
    if c == "c":
        return T["q" + buf][:, at:at + n].bitcast(dt.uint8)
    return T["p" + buf][:, at:at + n]


def make_eye(g, T):
    v, S = g.vector, T.sem
    v.memset(T.ones[:], 1.0).then_inc(S.ones, 1)
    v.memset(T.eye[:], 0.0).then_inc(S.zero, 1)
    g.wait_ge(S.ones, 1)
    g.affine_select(T.blk[:], T.ones[:], [[-1, NC]], AluOpType.is_equal, 0.0, 3, 4).then_inc(S.blk, 1)
    v.wait_ge(S.zero, 1)
    v.wait_ge(S.blk, 1)
    for i in range(4):
        v.tensor_copy(T.eye[32 * i:32 * i + 32, NC * i:NC * i + NC], T.blk[:]).then_inc(S.eye, 1)
    v.wait_ge(S.eye, 4)


def quant_s(g, T, b, sem):
    g.vector.quantize_mx(T.qs[:, b * NC:(b + 1) * NC], T.ps[:, b * NC:(b + 1) * NC], T.eye[:, 3 - b:3 - b + W]).then_inc(sem, 1)


def relay_core(g, core, r, k, T, topo, P):
    S, cores, far, lack = T.sem, T.cores, P[r]["far"], P[r]["lack"]
    eng = engines(topo, core, cores[far[0]])
    mask, n = sum(eng), len(eng)
    make_eye(g, T)
    quant_s(g, T, lack, S.k_s)
    g.wait_ge(S.k_s, 1)
    w = NC // 2 // RELAYS
    a = lack * NC + NC // 2 + k * w
    rid, pid, _ = topo.addr(cores[r])
    for c in "cp":
        g.remote_dma(part(T, c, "s", a, w), part(T, c, "s", a, w), S["as"], S.sent, pid, rid, mask)
    cnt = 2
    for o in CFG["gp"]:
        if o not in CFG["route"] or CFG["route"][o][0] != k:
            continue
        i, c = o[:-1], o[-1]
        g.wait_ge(S["r_" + o], len(engines(topo, cores[r], core)))
        for f in CFG["route"][o][1]:
            d = far[f]
            me = P[d]["far"].index(r)
            rid, pid, _ = topo.addr(cores[d])
            g.remote_dma(part(T, c, "l", (me + (2 if i == "h" else 0)) * NC), part(T, c, "r", ITEMS.index(i) * NC),
                         S["a%s%d" % (i[0], me)], S.sent, pid, rid, mask)
            cnt += 1
    g.wait_ge(S.sent, cnt * n)


def rank_core(g, core, rank, T, topo, P):
    S = T.sem
    near, far, nb, helpers, lack = [P[rank][k] for k in ("near", "far", "nb", "relays", "lack")]
    gift = P[nb]["lack"]
    v, s, t, y = g.vector, g.scalar, g.tensor, g.sync
    RELU, COPY = ActivationFunctionType.Relu, ActivationFunctionType.Copy
    e_nb = engines(topo, core, T.cores[nb])
    off = len(engines(topo, helpers[0], T.cores[far[0]]))
    bank = CFG["banks"]

    def cols(buf, i, n=1):
        return T[buf][:, i * NC:(i + n) * NC]

    every = list(range(4))
    source = {"a": (T.a, every), "bf": (T.b, far), "bp": (T.b, [nb, rank]), "w1": (T.w1, every), "x": (T.x, [0]), "w2": (T.w2, [0])}
    loads = CFG["sync"] + CFG["scalar"]
    quants = [o[1:] for o in CFG["vec"] if o[0] == "q"]
    tile = {"g0": 0, "g1": 1, "gn": 0, "go": 1, "h": 0}

    def piece(n, tile, pieces):
        return [(m, i) for m, i, k in pieces if m == n and i <= tile < i + k][0]

    def load(q, queue):
        for n, i, k in queue:
            src, at = source[n]
            q.dma_start(T["t" + n][:, i * W:(i + k) * W], src[:, at[i] * W:(at[i] + k) * W]).then_inc(S["l_%s%d" % (n, i)], 16)

    load(y, CFG["sync"])
    load(s, CFG["scalar"])
    make_eye(g, T)

    def result(q, n, b):
        q.wait_ge(S["m_%s%d" % (n, b)], 1)
        dst, src = T["t" + n][:, b:W:4], T[bank[n]][:, 512 * b:512 * b + NC]
        i = q.activation(dst, src, RELU, scale=FACTOR) if q is s else q.tensor_scalar(dst, src, 0.0, FACTOR, AluOpType.max, AluOpType.mult)
        i.then_inc(S["act_" + n], 1)

    rest = [b for b in range(4) if b not in (lack, gift)]
    for op in CFG["vec"]:
        n = op[1]
        if op[0] == "s":
            if n == "gift":
                quant_s(g, T, gift, S.k_gift)
            else:
                quant_s(g, T, rest[n], S.k_s)
        elif op[0] == "q":
            i, k = op[2:]
            for l in sorted({piece(n, j, loads) for j in range(i, i + k)}):
                v.wait_ge(S["l_%s%d" % l], 16)
            v.quantize_mx(cols("q" + n, i, k), cols("p" + n, i, k), T["t" + n][:, i * W:(i + k) * W]).then_inc(S["k_%s%d" % (n, i)], 1)
        elif op[0] == "r":
            result(v, n, op[2])
        else:
            buf, i = WHERE[n]
            v.wait_ge(S["act_" + n], 4)
            v.quantize_mx(cols("q" + buf, i), cols("p" + buf, i), T["t" + n][:]).then_inc(S["k_" + n], 1)
    for op in CFG["sca"]:
        result(s, op[1], op[2])

    def need(n, tile):
        t.wait_ge(S["k_%s%d" % piece(n, tile, quants)], 1)

    taken = {}

    def free(b):
        if b in taken:
            t.wait_ge(S["act_" + taken[b]], 4)

    D = {"own": ("k_go", 1, "go", 0), "nb": ("an", 2 * len(e_nb), "n", 1), "0": ("ag0", 2 * off, "l", 0), "1": ("ag1", 2 * off, "l", 1)}
    Y = {"own": ("k_h", 1, "o", 0), "nb": ("an", 2 * len(e_nb), "n", 0), "0": ("ah0", 2 * off, "l", 2), "1": ("ah1", 2 * off, "l", 3)}
    block = {"own": rank, "nb": nb, "0": far[0], "1": far[1]}
    sums = [o for o in CFG["ten"] if o[0] == "d"]
    prods = [o for o in CFG["ten"] if o[0] == "y"]
    for o in CFG["ten"]:
        kind, who = o.split()
        if kind == "L":
            w, m = LAYERS[who]
            i = tile[who]
            free(bank[who])
            taken[bank[who]] = who
            need(m, i)
            for b in range(4):
                need(w, b)
                t.matmul_mx(T[bank[who]][:, 512 * b:512 * b + NC], cols("q" + w, b), cols("p" + w, b), cols("q" + m, i), cols("p" + m, i),
                            True, True).then_inc(S["m_%s%d" % (who, b)], 1)
        elif kind == "d":
            if o == sums[0]:
                free(bank["z"])
                t.wait_ge(S.k_s, 2)
                t.wait_ge(S.k_gift, 1)
                t.wait_ge(S["as"], 2 * len(e_nb) + 2 * RELAYS * off)
            sem, n, buf, i = D[who]
            t.wait_ge(S[sem], n)
            for b in range(4):
                ins = t.matmul_mx(T[bank["z"]][:, 512 * b:512 * b + NC], cols("qs", b), cols("ps", b), cols("q" + buf, i), cols("p" + buf, i),
                                  o == sums[0], o == sums[-1])
                if o == sums[-1]:
                    ins.then_inc(S["m_z%d" % b], 1)
        else:
            if o == prods[0]:
                need("w2", 0)
                free(bank["y"])
            sem, n, buf, i = Y[who]
            k = block[who]
            t.wait_ge(S[sem], n)
            t.matmul_mx(T[bank["y"]][:, 512 * k:512 * k + NC], T.qw2[:], T.pw2[:], cols("q" + buf, i), cols("p" + buf, i),
                        True, True).then_inc(S["m_y%d" % k], 1)

    def out(q, sem, dst, src, done):
        q.wait_ge(sem, 1)
        (q.activation(dst, src, COPY) if q is s else q.tensor_copy(dst, src)).then_inc(done, 1)

    n_st, turn = 0, 0
    for o in CFG["ten"]:
        kind, who = o.split()
        if o == sums[-1]:
            for b in range(4):
                out((s, v)[b % 2], S["m_z%d" % b], T.zt[:, b:W:4], T[bank["z"]][:, 512 * b:512 * b + NC], S.cz)
            y.wait_ge(S.cz, 4)
            y.dma_start(T.z[:], T.zt[:]).then_inc(S.stored, 16)
            n_st += 1
        elif kind == "y":
            j, grp = [(j, grp) for j, grp in enumerate(CFG["ystore"]) if who in grp][0]
            k = block[who]
            out((v, s)[turn % 2], S["m_y%d" % k], cols("yt", k), T[bank["y"]][:, 512 * k:512 * k + NC], S["cy%d" % j])
            turn += 1
            if who == [p.split()[1] for p in prods if p.split()[1] in grp][-1]:
                a = min(block[w] for w in grp)
                y.wait_ge(S["cy%d" % j], len(grp))
                y.dma_start(T.y[:, a * NC:(a + len(grp)) * NC], cols("yt", a, len(grp))).then_inc(S.stored, 16)
                n_st += 1
    y.wait_ge(S.stored, 16 * n_st)

    for o in CFG["gp"]:
        i, c = o[:-1], o[-1]
        if o in CFG["route"]:
            to = helpers[CFG["route"][o][0]]
            done, arrive = ["k_" + i], "r_" + o
            buf, at = WHERE[i]
            src, dst = part(T, c, buf, at * NC), part(T, c, "r", ITEMS.index(i) * NC)
        elif i == "gift":
            to, done, arrive = T.cores[nb], ["k_gift"], "as"
            src = dst = part(T, c, "s", gift * NC, NC // 2)
        else:
            to, done, arrive = T.cores[nb], ["k_h", "k_gn"], "an"
            src, dst = part(T, c, "o", 0, 2 * NC), part(T, c, "n", 0, 2 * NC)
        for d in done:
            g.wait_ge(S[d], 1)
        rid, pid, _ = topo.addr(to)
        g.remote_dma(dst, src, S[arrive], S.sent, pid, rid, sum(engines(topo, core, to)))
    g.wait_ge(S.sent, len(CFG["gp"]) * len(e_nb))
